import numpy as np
import ml_dtypes

BF16 = ml_dtypes.bfloat16


def bf(x):
    return np.asarray(x, np.float32).astype(BF16)


def f32(x):
    return np.asarray(x, np.float32)


def f64(x):
    return np.asarray(x).astype(np.float64)


def striped(idx):
    return np.tile(idx.reshape(-1, 16).T, (8, 1))


S, K, M, N, D, V = 4096, 128, 128, 2048, 16, 128


def setup_inputs():
    return {"table": bf(np.random.standard_normal((K, S))), "w": bf(np.random.standard_normal((K, M)) / np.sqrt(K)), "b": f32(0.5 * np.random.standard_normal((M, 1))), "offs": striped(np.random.permutation(np.tile(np.arange(S), 2))[:N])}


def reference(table, w, b, offs):
    idx = offs[:16].T.reshape(-1)
    x = f64(table)[:, idx]
    y = f64(w).T @ x
    z = np.tanh(y + f64(b))
    return z.reshape(M, V, D).max(axis=2)

@@ -1,0 +1,42 @@
+import concourse.mybir as mybir
+
+BF16, F32, U16 = mybir.dt.bfloat16, mybir.dt.float32, mybir.dt.uint16
+
+P = 128
+S = 4096
+N = 2048
+D = 16
+PIECE = 512
+FLOPS = 2 * P * P * N
+
+
+def tile_gather_matmul_kernel(tc, table, w, b, offs, out):
+    nc = tc.nc
+    with (
+        tc.tile_pool(name="held", bufs=1) as held,
+        tc.psum_pool(name="psum", bufs=1) as psum,
+    ):
+        offsets = held.tile([P, N // 16], U16, name="offsets")
+        nc.sync.dma_start(offsets[:], offs)
+        nodes = held.tile([P, S], BF16, name="nodes")
+        nc.scalar.dma_start(nodes[:], table)
+        weights = held.tile([P, P], BF16, name="weights")
+        nc.sync.dma_start(weights[:], w)
+        bias = held.tile([P, 1], F32, name="bias")
+        nc.sync.dma_start(bias[:], b)
+
+        pooled = held.tile([P, N // D], F32, name="pooled")
+        for u in range(N // PIECE):
+            piece = offsets[:, u * (PIECE // 16) : (u + 1) * (PIECE // 16)]
+            bank = psum.tile([P, PIECE], F32, name=f"bank{u}")
+            nc.tensor.matmul(bank[:], weights[:], nodes[:].indirect(piece), start=True, stop=True)
+            nc.vector.tensor_reduce(
+                pooled[:, u * (PIECE // D) : (u + 1) * (PIECE // D)],
+                bank[:].rearrange("p (v t) -> p v t", t=D),
+                axis=mybir.AxisListType.X,
+                op=mybir.AluOpType.max,
+            )
+
+        result = held.tile([P, N // D], F32, name="result")
+        nc.scalar.activation(result[:], pooled[:], mybir.ActivationFunctionType.Tanh, bias=bias[:, 0:1])
+        nc.sync.dma_start(out, result[:])

@@ -7,6 +7,7 @@ S = 4096
 N = 2048
 D = 16
 PIECE = 512
+WARM_UPS = 8
 FLOPS = 2 * P * P * N
 
 
@@ -24,6 +25,12 @@ def tile_gather_matmul_kernel(tc, table, w, b, offs, out):
         nc.sync.dma_start(weights[:], w)
         bias = held.tile([P, 1], F32, name="bias")
         nc.sync.dma_start(bias[:], b)
+
+        zeros = held.tile([P, PIECE], BF16, name="zeros")
+        nc.vector.memset(zeros[:], 0.0)
+        unread = psum.tile([P, PIECE], F32, name="unread")
+        for i in range(WARM_UPS):
+            nc.tensor.matmul(unread[:], zeros[:, 0:P], zeros[:], start=True, stop=True)
 
         pooled = held.tile([P, N // D], F32, name="pooled")
         for u in range(N // PIECE):

@@ -7,7 +7,7 @@ S = 4096
 N = 2048
 D = 16
 PIECE = 512
-WARM_UPS = 8
+WARM_UPS, WARM_UP_COLUMNS = 8, 256
 FLOPS = 2 * P * P * N
 
 
@@ -26,9 +26,9 @@ def tile_gather_matmul_kernel(tc, table, w, b, offs, out):
         bias = held.tile([P, 1], F32, name="bias")
         nc.sync.dma_start(bias[:], b)
 
-        zeros = held.tile([P, PIECE], BF16, name="zeros")
+        zeros = held.tile([P, WARM_UP_COLUMNS], BF16, name="zeros")
         nc.vector.memset(zeros[:], 0.0)
-        unread = psum.tile([P, PIECE], F32, name="unread")
+        unread = psum.tile([P, WARM_UP_COLUMNS], F32, name="unread")
         for i in range(WARM_UPS):
             nc.tensor.matmul(unread[:], zeros[:, 0:P], zeros[:], start=True, stop=True)
 

@@ -6,8 +6,8 @@ P = 128
 S = 4096
 N = 2048
 D = 16
-PIECE = 512
-WARM_UPS, WARM_UP_COLUMNS = 8, 256
+PIECE = 256
+PIECES = N // PIECE
 FLOPS = 2 * P * P * N
 
 
@@ -15,7 +15,7 @@ def tile_gather_matmul_kernel(tc, table, w, b, offs, out):
     nc = tc.nc
     with (
         tc.tile_pool(name="held", bufs=1) as held,
-        tc.psum_pool(name="psum", bufs=1) as psum,
+        tc.psum_pool(name="psum", bufs=PIECES) as psum,
     ):
         offsets = held.tile([P, N // 16], U16, name="offsets")
         nc.sync.dma_start(offsets[:], offs)
@@ -26,24 +26,23 @@ def tile_gather_matmul_kernel(tc, table, w, b, offs, out):
         bias = held.tile([P, 1], F32, name="bias")
         nc.sync.dma_start(bias[:], b)
 
-        zeros = held.tile([P, WARM_UP_COLUMNS], BF16, name="zeros")
-        nc.vector.memset(zeros[:], 0.0)
-        unread = psum.tile([P, WARM_UP_COLUMNS], F32, name="unread")
-        for i in range(WARM_UPS):
-            nc.tensor.matmul(unread[:], zeros[:, 0:P], zeros[:], start=True, stop=True)
-
         pooled = held.tile([P, N // D], F32, name="pooled")
-        for u in range(N // PIECE):
+        result = held.tile([P, N // D], F32, name="result")
+        for u in range(PIECES):
             piece = offsets[:, u * (PIECE // 16) : (u + 1) * (PIECE // 16)]
-            bank = psum.tile([P, PIECE], F32, name=f"bank{u}")
+            pooled_nodes = slice(u * (PIECE // D), (u + 1) * (PIECE // D))
+            bank = psum.tile([P, PIECE], F32, name="bank")
             nc.tensor.matmul(bank[:], weights[:], nodes[:].indirect(piece), start=True, stop=True)
             nc.vector.tensor_reduce(
-                pooled[:, u * (PIECE // D) : (u + 1) * (PIECE // D)],
+                pooled[:, pooled_nodes],
                 bank[:].rearrange("p (v t) -> p v t", t=D),
                 axis=mybir.AxisListType.X,
                 op=mybir.AluOpType.max,
             )
-
-        result = held.tile([P, N // D], F32, name="result")
-        nc.scalar.activation(result[:], pooled[:], mybir.ActivationFunctionType.Tanh, bias=bias[:, 0:1])
-        nc.sync.dma_start(out, result[:])
+            nc.scalar.activation(
+                result[:, pooled_nodes],
+                pooled[:, pooled_nodes],
+                mybir.ActivationFunctionType.Tanh,
+                bias=bias[:, 0:1],
+            )
+        nc.scalar.dma_start(out, result[:])

@@ -8,6 +8,7 @@ N = 2048
 D = 16
 PIECE = 256
 PIECES = N // PIECE
+EARLY_NODES = (PIECES - 1) * (PIECE // D)
 FLOPS = 2 * P * P * N
 
 
@@ -27,7 +28,8 @@ def tile_gather_matmul_kernel(tc, table, w, b, offs, out):
         nc.sync.dma_start(bias[:], b)
 
         pooled = held.tile([P, N // D], F32, name="pooled")
-        result = held.tile([P, N // D], F32, name="result")
+        early = held.tile([P, EARLY_NODES], F32, name="early")
+        last = held.tile([P, PIECE // D], F32, name="last")
         for u in range(PIECES):
             piece = offsets[:, u * (PIECE // 16) : (u + 1) * (PIECE // 16)]
             pooled_nodes = slice(u * (PIECE // D), (u + 1) * (PIECE // D))
@@ -40,9 +42,11 @@ def tile_gather_matmul_kernel(tc, table, w, b, offs, out):
                 op=mybir.AluOpType.max,
             )
             nc.scalar.activation(
-                result[:, pooled_nodes],
+                early[:, pooled_nodes] if u < PIECES - 1 else last[:],
                 pooled[:, pooled_nodes],
                 mybir.ActivationFunctionType.Tanh,
                 bias=bias[:, 0:1],
             )
-        nc.scalar.dma_start(out, result[:])
+            if u == PIECES - 2:
+                nc.sync.dma_start(out[:, 0:EARLY_NODES], early[:])
+        nc.scalar.dma_start(out[:, EARLY_NODES : N // D], last[:])

@@ -27,6 +27,10 @@ def tile_gather_matmul_kernel(tc, table, w, b, offs, out):
         bias = held.tile([P, 1], F32, name="bias")
         nc.sync.dma_start(bias[:], b)
 
+        scratch = held.tile([P, 1], F32, name="scratch")
+        nc.vector.memset(scratch[:], 0.0)
+        nc.scalar.activation(scratch[:], scratch[:], mybir.ActivationFunctionType.Tanh)
+
         pooled = held.tile([P, N // D], F32, name="pooled")
         early = held.tile([P, EARLY_NODES], F32, name="early")
         last = held.tile([P, PIECE // D], F32, name="last")

import concourse.mybir as mybir

BF16, F32, U16 = mybir.dt.bfloat16, mybir.dt.float32, mybir.dt.uint16

P = 128
S = 4096
N = 2048
D = 16
PIECE = 256
PIECES = N // PIECE
EARLY_NODES = (PIECES - 1) * (PIECE // D)
FLOPS = 2 * P * P * N


def tile_gather_matmul_kernel(tc, table, w, b, offs, out):
    nc = tc.nc
    with (
        tc.tile_pool(name="held", bufs=1) as held,
        tc.psum_pool(name="psum", bufs=PIECES) as psum,
    ):
        offsets = held.tile([P, N // 16], U16, name="offsets")
        nc.sync.dma_start(offsets[:], offs)
        nodes = held.tile([P, S], BF16, name="nodes")
        nc.scalar.dma_start(nodes[:], table)
        weights = held.tile([P, P], BF16, name="weights")
        nc.sync.dma_start(weights[:], w)
        bias = held.tile([P, 1], F32, name="bias")
        nc.sync.dma_start(bias[:], b)

        scratch = held.tile([P, 1], F32, name="scratch")
        nc.vector.memset(scratch[:], 0.0)
        nc.scalar.activation(scratch[:], scratch[:], mybir.ActivationFunctionType.Tanh)

        pooled = held.tile([P, N // D], F32, name="pooled")
        early = held.tile([P, EARLY_NODES], F32, name="early")
        last = held.tile([P, PIECE // D], F32, name="last")
        for u in range(PIECES):
            piece = offsets[:, u * (PIECE // 16) : (u + 1) * (PIECE // 16)]
            pooled_nodes = slice(u * (PIECE // D), (u + 1) * (PIECE // D))
            bank = psum.tile([P, PIECE], F32, name="bank")
            nc.tensor.matmul(bank[:], weights[:], nodes[:].indirect(piece), start=True, stop=True)
            nc.vector.tensor_reduce(
                pooled[:, pooled_nodes],
                bank[:].rearrange("p (v t) -> p v t", t=D),
                axis=mybir.AxisListType.X,
                op=mybir.AluOpType.max,
            )
            nc.scalar.activation(
                early[:, pooled_nodes] if u < PIECES - 1 else last[:],
                pooled[:, pooled_nodes],
                mybir.ActivationFunctionType.Tanh,
                bias=bias[:, 0:1],
            )
            if u == PIECES - 2:
                nc.sync.dma_start(out[:, 0:EARLY_NODES], early[:])
        nc.scalar.dma_start(out[:, EARLY_NODES : N // D], last[:])
